import numpy as np
import ml_dtypes


def mxq(x, axis, fmt="e4m3"):
    dtype, down = {"e4m3": (ml_dtypes.float8_e4m3fn, 7), "e5m2": (ml_dtypes.float8_e5m2, 14)}[fmt]
    v = np.moveaxis(np.asarray(x, np.float32).astype(ml_dtypes.bfloat16).astype(np.float64), axis, -1)
    blocks = v.reshape(v.shape[:-1] + (-1, 32))
    amax = np.abs(blocks).max(-1, keepdims=True)
    byte = np.maximum(np.where(amax > 0, np.frexp(amax)[1] - 1 + 127, 0) - down, 1)
    scale = np.exp2(byte - 127.0)
    codes = (blocks / scale).astype(np.float32).astype(dtype).astype(np.float64)
    return np.moveaxis((codes * scale).reshape(v.shape), -1, axis)


WIDE = False


def mx_kscale(k):
    if not WIDE:
        return np.ones(k)
    levels = np.array([10, -10, 5, -5, 0])
    if k % 512:
        return np.exp2(np.random.permutation(np.resize(levels, k // 32))).repeat(32)
    a = np.empty((k // 512, 16))
    for p in range(k // 512):
        a[p, :8] = np.random.permutation(np.resize(levels, 8))
        for g in range(8):
            far = levels[np.abs(levels - a[p, g]) >= 10]
            a[p, g + 8] = far[np.random.randint(len(far))]
    return np.exp2(a.ravel()).repeat(32)


def f64(x):
    return np.asarray(x).astype(np.float64)


def striped(idx):
    return np.tile(np.asarray(idx).reshape(-1, 16).T, (8, 1)).astype(np.uint16)


def unstriped(offs):
    return offs[:16].T.reshape(-1).astype(np.int64)


E2M1 = np.array([0.0, 0.5, 1.0, 1.5, 2.0, 3.0, 4.0, 6.0, -0.0, -0.5, -1.0, -1.5, -2.0, -3.0, -4.0, -6.0])


def pack_weight(w, fmt):
    k, n = w.shape
    w = f64(np.asarray(w, np.float32).astype(ml_dtypes.bfloat16)).reshape(k // 32, 32, n)
    amax = np.abs(w).max(1)
    if fmt == "e4m3":
        byte = np.frexp(amax)[1] - 1 + 127 - 7
    else:
        mant, ex = np.frexp(amax / 6.0)
        byte = np.where(mant > 0.5, ex, ex - 1) + 127
    byte = np.clip(np.where(amax > 0, byte, 1), 1, 254)
    scaled = (w * np.exp2(127.0 - byte)[:, None, :]).reshape(k, n).astype(np.float32)
    by_word = np.ascontiguousarray(scaled.reshape(k // 512, 128, 4, n).transpose(0, 1, 3, 2))
    if fmt == "e4m3":
        words = by_word.astype(ml_dtypes.float8_e4m3fn).view(np.uint8)
    else:
        c = by_word.astype(ml_dtypes.float4_e2m1fn).view(np.uint8) & 0xF
        words = (c[..., 0::2] | (c[..., 1::2] << 4)).reshape(k // 512, 128, 2 * n)
    return np.ascontiguousarray(words), np.ascontiguousarray(byte.astype(np.uint8).reshape(k // 512, 16, n))


def unpack_weight(words, scales, fmt):
    g, _, n = scales.shape
    words = np.ascontiguousarray(words).reshape(g, 128, n, -1)
    if fmt == "e4m3":
        vals = words.view(ml_dtypes.float8_e4m3fn).astype(np.float64)
    else:
        nib = np.empty((g, 128, n, 4), np.uint8)
        nib[..., 0::2] = words & 0xF
        nib[..., 1::2] = words >> 4
        vals = E2M1[nib]
    vals = vals * np.repeat(np.exp2(scales.astype(np.float64) - 127.0), 8, axis=1)[..., None]
    return vals.transpose(0, 1, 3, 2).reshape(g * 512, n)


D, E, T, I, Q = 512, 512, 2048, 512, 128


def setup_inputs():
    n = np.random.standard_normal
    idx = np.random.permutation(T)[:I]
    fd = mx_kscale(D)
    fe = mx_kscale(E)
    keysp = pack_weight(n((D, T)) / fd[:, None], "e2m1")
    valsp = pack_weight(n((E, T)) / fe[:, None], "e2m1")
    return {
        "query": (n((D, Q)) * 0.8 / np.sqrt(D) * fd[:, None]).astype(np.float32),
        "keys_words": keysp[0],
        "keys_scales": keysp[1],
        "lean": (np.random.uniform(0.2, 0.6, (Q, 1))).astype(np.float32),
        "gout": (n((E, Q)) * 1 / np.sqrt(E) * fe[:, None]).astype(np.float32),
        "vals_words": valsp[0],
        "vals_scales": valsp[1],
        "base": (0.5 * n((Q, I))).astype(np.float32),
        "offs": striped(idx),
    }


def reference(query, keys_words, keys_scales, lean, gout, vals_words, vals_scales, base, offs):
    idx = unstriped(offs)
    keysu = unpack_weight(keys_words, keys_scales, "e2m1")
    valsu = unpack_weight(vals_words, vals_scales, "e2m1")
    queryq = mxq(f64(query), 0, "e4m3")
    keysidxg = keysu[:, idx]
    a = queryq.T @ keysidxg
    p = np.exp(a - np.max(a, axis=1, keepdims=True))
    r = p / np.sum(p, axis=1, keepdims=True)
    m0 = np.sum(r * a, axis=1, keepdims=True)
    goutq = mxq(f64(gout), 0, "e4m3")
    valsidxg = valsu[:, idx]
    c0 = goutq.T @ valsidxg
    dm0 = np.sum(c0 * r * f64(lean) * (-1.0), axis=1, keepdims=True)
    dr = c0 * ((a - m0) * f64(lean) + 1.0) + dm0 * a
    dp = dr / np.sum(p, axis=1, keepdims=True) + np.sum(dr * p / np.square(np.sum(p, axis=1, keepdims=True)) * (-1.0), axis=1, keepdims=True)
    da = c0 * r * f64(lean) + dm0 * r + dp * p
    hda = da * 512.0 * 2.0 * 512.0
    hdp = hda * p
    hdr = hdp / np.sum(p, axis=1, keepdims=True) + np.sum(hdp, axis=1, keepdims=True) * (-1.0) / np.square(np.sum(p, axis=1, keepdims=True)) * p
    hdm0 = np.sum(hda * r, axis=1, keepdims=True) + np.sum(hdr * a, axis=1, keepdims=True)
    hm0 = np.sum(hdr * c0 * f64(lean) * (-1.0), axis=1, keepdims=True)
    hr = hda * f64(lean) * c0 + hda * dm0 + hdm0 * (-1.0) * f64(lean) * c0 + hm0 * a
    hp = hda * dp + np.sum(hdp * dr / np.square(np.sum(p, axis=1, keepdims=True)) * (-1.0), axis=1, keepdims=True) + np.sum(hdp, axis=1, keepdims=True) * (-1.0) / np.square(np.sum(p, axis=1, keepdims=True)) * dr + np.sum(np.sum(hdp, axis=1, keepdims=True) * (-1.0) * dr * p / np.square(np.square(np.sum(p, axis=1, keepdims=True))) * (-1.0), axis=1, keepdims=True) * np.sum(p, axis=1, keepdims=True) * 2.0 + hr / np.sum(p, axis=1, keepdims=True) + np.sum(hr * p / np.square(np.sum(p, axis=1, keepdims=True)) * (-1.0), axis=1, keepdims=True)
    ha = hdr * c0 * f64(lean) + hdr * dm0 + hm0 * r + hp * p
    y = ha + f64(base)
    return y

@@ -1,0 +1,191 @@
+import math
+from contextlib import ExitStack
+
+import concourse.mybir as mybir
+
+D, E, T, I, Q = 512, 512, 2048, 512, 128
+FLOPS = 2 * Q * I * (D + E)
+
+F32 = mybir.dt.float32
+BF16 = mybir.dt.bfloat16
+I32 = mybir.dt.int32
+U32 = mybir.dt.uint32
+U16 = mybir.dt.uint16
+U8 = mybir.dt.uint8
+FP8X4 = mybir.dt.float8_e4m3fn_x4
+FP4X4 = mybir.dt.float4_e2m1fn_x4
+ALU = mybir.AluOpType
+ACT = mybir.ActivationFunctionType
+AX = mybir.AxisListType
+
+P = 128
+PACK = 4
+PENALTY = 2.0 * 512.0 * 512.0
+ROOT = math.sqrt(PENALTY)
+
+
+def tile_attend_gpdirect_leaning_kernel(
+    tc, query, keys_words, keys_scales, lean, gout, vals_words, vals_scales, base, offs, out
+):
+    nc = tc.nc
+    with ExitStack() as ctx:
+        keep = ctx.enter_context(tc.tile_pool(name="keep", bufs=1))
+        psum = ctx.enter_context(tc.psum_pool(name="psum", bufs=1))
+
+        def wide(name):
+            return keep.tile([P, I], F32, name=name, align_bytes=64)
+
+        def column(name):
+            return keep.tile([P, 1], F32, name=name)
+
+        def scale_window(name):
+            window = keep.tile([P, T], U8, name=name, align_bytes=64)
+            nc.vector.memset(window[:].bitcast(I32), 0)
+            return window
+
+        def load_scales(queue, window, scales):
+            rows = scales[0].bitcast(I32)
+            for quadrant in range(4):
+                queue.dma_start(
+                    out=window[32 * quadrant : 32 * quadrant + 4, :].bitcast(I32),
+                    in_=rows[4 * quadrant : 4 * quadrant + 4, :],
+                )
+
+        def load_words(name, words):
+            window = keep.tile([P, T], U16, name=name, align_bytes=64)
+            nc.sync.dma_start(out=window[:].bitcast(I32), in_=words[0].bitcast(I32))
+            return window
+
+        def load_rows(name, rows):
+            raw = keep.tile([P, PACK * Q], F32, name=name, tag="staged", align_bytes=64)
+            nc.sync.dma_start(out=raw[:], in_=rows.rearrange("(p t) q -> p (t q)", t=PACK))
+            return raw
+
+        def interleave(name, raw):
+            grouped = keep.tile([P, Q, PACK], BF16, name=name, align_bytes=64)
+            nc.scalar.copy(out=grouped[:], in_=raw[:].rearrange("p (t q) -> p q t", t=PACK))
+            return grouped
+
+        def quantize(name, grouped):
+            codes = keep.tile([P, Q], U32, name=name + "_codes", align_bytes=64)
+            scales = keep.tile([P, Q], U8, name=name + "_scales", align_bytes=64)
+            nc.vector.quantize_mx(
+                out=codes[:].bitcast(FP8X4), scales=scales[:], in_=grouped[:].rearrange("p q t -> p (q t)")
+            )
+            return codes, scales
+
+        def gather(name, window, dtype):
+            picked = keep.tile([P, I], dtype, name=name, align_bytes=64)
+            nc.vector.tensor_copy(picked[:], window[:].indirect(offsets[:]))
+            return picked
+
+        def product(name, rows, words, scales):
+            bank = psum.tile([P, I], F32, name=name)
+            nc.tensor.matmul_mx(
+                out=bank[:], lhsT=rows[0][:].bitcast(FP8X4), lhsT_scale=rows[1][:],
+                rhs=words[:].bitcast(FP4X4), rhs_scale=scales[:], start=True, stop=True,
+            )
+            return bank
+
+        def fused(out_tile, in0, scalar, in1, op0, op1, total=None, cols=slice(0, I)):
+            nc.vector.scalar_tensor_tensor(
+                out=out_tile[:, cols], in0=in0[:, cols], scalar=scalar, in1=in1[:, cols], op0=op0, op1=op1,
+                accum_out=None if total is None else total[:],
+            )
+
+        def affine(name, x, scale, bias):
+            y = column(name)
+            nc.scalar.activation(out=y[:], in_=x[:], func=ACT.Identity, scale=scale, bias=bias)
+            return y
+
+        def scaled(name, x, scale):
+            y = column(name)
+            nc.scalar.activation(out=y[:], in_=x[:], func=ACT.Copy, scale=scale)
+            return y
+
+        ks_window = scale_window("ks_window")
+        vs_window = scale_window("vs_window")
+
+        offsets = keep.tile([P, I // 16], U16, name="offsets")
+        nc.sync.dma_start(offsets[:], offs)
+        kw_window = load_words("kw_window", keys_words)
+        load_scales(nc.scalar, ks_window, keys_scales)
+        q_raw = load_rows("q_raw", query)
+        vw_window = load_words("vw_window", vals_words)
+        load_scales(nc.sync, vs_window, vals_scales)
+        l = column("l")
+        nc.gpsimd.dma_start(out=l[:], in_=lean)
+        l_plus_1 = column("l_plus_1")
+        nc.gpsimd.tensor_scalar(l_plus_1[:], l[:], 1.0, 1.0, ALU.mult, ALU.add)
+        l_2root = column("l_2root")
+        nc.gpsimd.tensor_scalar(l_2root[:], l[:], 2.0 * ROOT, 0.0, ALU.mult, ALU.add)
+
+        q_grouped = interleave("q_grouped", q_raw)
+        g_raw = load_rows("g_raw", gout)
+        g_grouped = interleave("g_grouped", g_raw)
+        base_sb = keep.tile([P, PACK * Q], F32, name="base_sb", tag="staged", align_bytes=64)
+        nc.sync.dma_start(out=base_sb[:], in_=base)
+
+        kw = gather("kw", kw_window, U16)
+        ks = gather("ks", ks_window, U8)
+        q_mx = quantize("q", q_grouped)
+        a = product("a", q_mx, kw, ks)
+        vw = gather("vw", vw_window, U16)
+
+        neg_max = column("neg_max")
+        nc.vector.tensor_reduce(out=neg_max[:], in_=a[:], axis=AX.X, op=ALU.max, negate=True)
+        p, p_sum = wide("p"), column("p_sum")
+        nc.scalar.activation(out=p[:], in_=a[:], func=ACT.Exp, bias=neg_max[:], scale=1.0, accum_out=p_sum[:])
+        la = wide("la")
+        nc.scalar.activation(out=la[:], in_=a[:], func=ACT.Copy, scale=l[:])
+
+        g_mx = quantize("g", g_grouped)
+        vs = gather("vs", vs_window, U8)
+        c = product("c", g_mx, vw, vs)
+
+        inv_sum = column("inv_sum")
+        nc.vector.reciprocal(out=inv_sum[:], in_=p_sum[:])
+        r = wide("r")
+        nc.scalar.activation(out=r[:], in_=p[:], func=ACT.Copy, scale=inv_sum[:])
+
+        spare = wide("spare")
+        neg_pla = column("neg_pla")
+        fused(spare, la, -1.0, p, ALU.mult, ALU.mult, neg_pla)
+        w_shift = affine("w_shift", neg_pla, inv_sum[:], l_plus_1[:])
+        rc, c_mean = wide("rc"), column("c_mean")
+        fused(rc, c, inv_sum[:], p, ALU.mult, ALU.mult, c_mean)
+        rw = wide("rw")
+        fused(rw, la, w_shift[:], r, ALU.add, ALU.mult)
+        rvw, vw_mean = wide("rvw"), column("vw_mean")
+        fused(rvw, c, c_mean[:], rw, ALU.subtract, ALU.mult, vw_mean)
+        neg_da = wide("neg_da")
+        fused(neg_da, r, vw_mean[:], rvw, ALU.mult, ALU.subtract)
+
+        rh, b = wide("rh"), column("b")
+        fused(rh, neg_da, -0.5 * ROOT, r, ALU.mult, ALU.mult, b)
+        spare2, gh = wide("spare2"), column("gh")
+        nc.scalar.activation(out=spare2[:], in_=neg_da[:], func=ACT.Square, scale=ROOT, accum_out=gh[:])
+        spare3, neg_hw = wide("spare3"), column("neg_hw")
+        fused(spare3, neg_da, PENALTY, rw, ALU.mult, ALU.mult, neg_hw)
+        square = wide("square")
+        nc.scalar.activation(out=square[:], in_=neg_da[:], func=ACT.Square, scale=ROOT, bias=b[:])
+        rhv, hv = wide("rhv"), column("hv")
+        fused(rhv, c, c_mean[:], rh, ALU.subtract, ALU.mult, hv)
+
+        k_rc = affine("k_rc", b, 2.0 * ROOT, neg_hw[:])
+        t1 = affine("t1", k_rc, c_mean[:], gh[:])
+        neg_t1 = scaled("neg_t1", t1, -1.0)
+        b_squared = scaled("b_squared", b, b[:])
+        k_rw = scaled("k_rw", hv, -2.0 * ROOT)
+        k_r = affine("k_r", hv, 2.0 * ROOT, neg_t1[:])
+
+        left0, right0, left1, right1, result = (wide(n) for n in ("left0", "right0", "left1", "right1", "result"))
+        fused(left0, rc, k_rc[:], base_sb, ALU.mult, ALU.add)
+        fused(right0, rhv, l_2root[:], square, ALU.mult, ALU.add)
+        fused(left1, rw, k_rw[:], left0, ALU.mult, ALU.add)
+        halves = (slice(0, I // 2), slice(I // 2, I))
+        for cols in halves:
+            fused(right1, r, k_r[:], right0, ALU.mult, ALU.add, cols=cols)
+        for cols, queue in zip(halves, (nc.sync, nc.scalar)):
+            fused(result, left1, b_squared[:], right1, ALU.subtract, ALU.add, cols=cols)
+            queue.dma_start(out=out[:, cols], in_=result[:, cols])

@@ -38,9 +38,9 @@ def tile_attend_gpdirect_leaning_kernel(
         def column(name):
             return keep.tile([P, 1], F32, name=name)
 
-        def scale_window(name):
+        def scale_window(name, engine):
             window = keep.tile([P, T], U8, name=name, align_bytes=64)
-            nc.vector.memset(window[:].bitcast(I32), 0)
+            engine.memset(window[:].bitcast(I32), 0)
             return window
 
         def load_scales(queue, window, scales):
@@ -57,12 +57,12 @@ def tile_attend_gpdirect_leaning_kernel(
             return window
 
         def load_rows(name, rows):
-            raw = keep.tile([P, PACK * Q], F32, name=name, tag="staged", align_bytes=64)
+            raw = keep.tile([P, PACK * Q], F32, name=name, tag=name, align_bytes=64)
             nc.sync.dma_start(out=raw[:], in_=rows.rearrange("(p t) q -> p (t q)", t=PACK))
             return raw
 
         def interleave(name, raw):
-            grouped = keep.tile([P, Q, PACK], BF16, name=name, align_bytes=64)
+            grouped = keep.tile([P, Q, PACK], BF16, name=name, tag=name, align_bytes=64)
             nc.scalar.copy(out=grouped[:], in_=raw[:].rearrange("p (t q) -> p q t", t=PACK))
             return grouped
 
@@ -74,8 +74,8 @@ def tile_attend_gpdirect_leaning_kernel(
             )
             return codes, scales
 
-        def gather(name, window, dtype):
-            picked = keep.tile([P, I], dtype, name=name, align_bytes=64)
+        def gather(name, window, dtype, tag):
+            picked = keep.tile([P, I], dtype, name=name, tag=tag, align_bytes=64)
             nc.vector.tensor_copy(picked[:], window[:].indirect(offsets[:]))
             return picked
 
@@ -103,34 +103,34 @@ def tile_attend_gpdirect_leaning_kernel(
             nc.scalar.activation(out=y[:], in_=x[:], func=ACT.Copy, scale=scale)
             return y
 
-        ks_window = scale_window("ks_window")
-        vs_window = scale_window("vs_window")
+        ks_window = scale_window("ks_window", nc.vector)
+        vs_window = scale_window("vs_window", nc.vector)
 
         offsets = keep.tile([P, I // 16], U16, name="offsets")
-        nc.sync.dma_start(offsets[:], offs)
         kw_window = load_words("kw_window", keys_words)
-        load_scales(nc.scalar, ks_window, keys_scales)
+        nc.sync.dma_start(offsets[:], offs)
+        load_scales(nc.sync, ks_window, keys_scales)
         q_raw = load_rows("q_raw", query)
         vw_window = load_words("vw_window", vals_words)
+        g_raw = load_rows("g_raw", gout)
         load_scales(nc.sync, vs_window, vals_scales)
         l = column("l")
-        nc.gpsimd.dma_start(out=l[:], in_=lean)
+        nc.sync.dma_start(out=l[:], in_=lean)
         l_plus_1 = column("l_plus_1")
         nc.gpsimd.tensor_scalar(l_plus_1[:], l[:], 1.0, 1.0, ALU.mult, ALU.add)
         l_2root = column("l_2root")
         nc.gpsimd.tensor_scalar(l_2root[:], l[:], 2.0 * ROOT, 0.0, ALU.mult, ALU.add)
 
         q_grouped = interleave("q_grouped", q_raw)
-        g_raw = load_rows("g_raw", gout)
-        g_grouped = interleave("g_grouped", g_raw)
-        base_sb = keep.tile([P, PACK * Q], F32, name="base_sb", tag="staged", align_bytes=64)
+        base_sb = keep.tile([P, PACK * Q], F32, name="base_sb", tag="q_raw", align_bytes=64)
         nc.sync.dma_start(out=base_sb[:], in_=base)
+        g_grouped = interleave("g_grouped", g_raw)
 
-        kw = gather("kw", kw_window, U16)
-        ks = gather("ks", ks_window, U8)
+        kw = gather("kw", kw_window, U16, "kw")
+        ks = gather("ks", ks_window, U8, "ks")
         q_mx = quantize("q", q_grouped)
         a = product("a", q_mx, kw, ks)
-        vw = gather("vw", vw_window, U16)
+        vw = gather("vw", vw_window, U16, "q_grouped")
 
         neg_max = column("neg_max")
         nc.vector.tensor_reduce(out=neg_max[:], in_=a[:], axis=AX.X, op=ALU.max, negate=True)
@@ -140,7 +140,7 @@ def tile_attend_gpdirect_leaning_kernel(
         nc.scalar.activation(out=la[:], in_=a[:], func=ACT.Copy, scale=l[:])
 
         g_mx = quantize("g", g_grouped)
-        vs = gather("vs", vs_window, U8)
+        vs = gather("vs", vs_window, U8, "ks")
         c = product("c", g_mx, vw, vs)
 
         inv_sum = column("inv_sum")
@@ -148,11 +148,10 @@ def tile_attend_gpdirect_leaning_kernel(
         r = wide("r")
         nc.scalar.activation(out=r[:], in_=p[:], func=ACT.Copy, scale=inv_sum[:])
 
-        spare = wide("spare")
-        neg_pla = column("neg_pla")
-        fused(spare, la, -1.0, p, ALU.mult, ALU.mult, neg_pla)
-        w_shift = affine("w_shift", neg_pla, inv_sum[:], l_plus_1[:])
         rc, c_mean = wide("rc"), column("c_mean")
+        neg_pla = column("neg_pla")
+        fused(rc, la, -1.0, p, ALU.mult, ALU.mult, neg_pla)
+        w_shift = affine("w_shift", neg_pla, inv_sum[:], l_plus_1[:])
         fused(rc, c, inv_sum[:], p, ALU.mult, ALU.mult, c_mean)
         rw = wide("rw")
         fused(rw, la, w_shift[:], r, ALU.add, ALU.mult)

@@ -16,7 +16,6 @@ FP8X4 = mybir.dt.float8_e4m3fn_x4
 FP4X4 = mybir.dt.float4_e2m1fn_x4
 ALU = mybir.AluOpType
 ACT = mybir.ActivationFunctionType
-AX = mybir.AxisListType
 
 P = 128
 PACK = 4
@@ -74,17 +73,20 @@ def tile_attend_gpdirect_leaning_kernel(
             )
             return codes, scales
 
-        def gather(name, window, dtype, tag):
+        def gather(name, window, dtype, tag, parts):
             picked = keep.tile([P, I], dtype, name=name, tag=tag, align_bytes=64)
-            nc.vector.tensor_copy(picked[:], window[:].indirect(offsets[:]))
+            for cols in parts:
+                entries = offsets[:, cols.start // 16 : cols.stop // 16]
+                nc.vector.tensor_copy(picked[:, cols], window[:].indirect(entries))
             return picked
 
-        def product(name, rows, words, scales):
+        def product(name, rows, words, scales, parts):
             bank = psum.tile([P, I], F32, name=name)
-            nc.tensor.matmul_mx(
-                out=bank[:], lhsT=rows[0][:].bitcast(FP8X4), lhsT_scale=rows[1][:],
-                rhs=words[:].bitcast(FP4X4), rhs_scale=scales[:], start=True, stop=True,
-            )
+            for cols in parts:
+                nc.tensor.matmul_mx(
+                    out=bank[:, cols], lhsT=rows[0][:].bitcast(FP8X4), lhsT_scale=rows[1][:],
+                    rhs=words[:, cols].bitcast(FP4X4), rhs_scale=scales[:, cols], start=True, stop=True,
+                )
             return bank
 
         def fused(out_tile, in0, scalar, in1, op0, op1, total=None, cols=slice(0, I)):
@@ -103,6 +105,8 @@ def tile_attend_gpdirect_leaning_kernel(
             nc.scalar.activation(out=y[:], in_=x[:], func=ACT.Copy, scale=scale)
             return y
 
+        whole = (slice(0, I),)
+        halves = (slice(0, I // 2), slice(I // 2, I))
         ks_window = scale_window("ks_window", nc.vector)
         vs_window = scale_window("vs_window", nc.vector)
 
@@ -126,22 +130,23 @@ def tile_attend_gpdirect_leaning_kernel(
         nc.sync.dma_start(out=base_sb[:], in_=base)
         g_grouped = interleave("g_grouped", g_raw)
 
-        kw = gather("kw", kw_window, U16, "kw")
-        ks = gather("ks", ks_window, U8, "ks")
+        kw = gather("kw", kw_window, U16, "kw", whole)
+        ks = gather("ks", ks_window, U8, "ks", whole)
         q_mx = quantize("q", q_grouped)
-        a = product("a", q_mx, kw, ks)
-        vw = gather("vw", vw_window, U16, "q_grouped")
+        a = product("a", q_mx, kw, ks, whole)
+        vw = gather("vw", vw_window, U16, "q_grouped", whole)
 
         neg_max = column("neg_max")
-        nc.vector.tensor_reduce(out=neg_max[:], in_=a[:], axis=AX.X, op=ALU.max, negate=True)
+        neg_a = wide("neg_a")
+        nc.vector.tensor_scalar(neg_a[:], a[:], -1.0, None, ALU.mult, ALU.min, accum_out=neg_max[:])
         p, p_sum = wide("p"), column("p_sum")
         nc.scalar.activation(out=p[:], in_=a[:], func=ACT.Exp, bias=neg_max[:], scale=1.0, accum_out=p_sum[:])
         la = wide("la")
         nc.scalar.activation(out=la[:], in_=a[:], func=ACT.Copy, scale=l[:])
 
         g_mx = quantize("g", g_grouped)
-        vs = gather("vs", vs_window, U8, "ks")
-        c = product("c", g_mx, vw, vs)
+        vs = gather("vs", vs_window, U8, "ks", halves)
+        c = product("c", g_mx, vw, vs, halves)
 
         inv_sum = column("inv_sum")
         nc.vector.reciprocal(out=inv_sum[:], in_=p_sum[:])
@@ -150,7 +155,7 @@ def tile_attend_gpdirect_leaning_kernel(
 
         rc, c_mean = wide("rc"), column("c_mean")
         neg_pla = column("neg_pla")
-        fused(rc, la, -1.0, p, ALU.mult, ALU.mult, neg_pla)
+        fused(rc, neg_a, l[:], p, ALU.mult, ALU.mult, neg_pla)
         w_shift = affine("w_shift", neg_pla, inv_sum[:], l_plus_1[:])
         fused(rc, c, inv_sum[:], p, ALU.mult, ALU.mult, c_mean)
         rw = wide("rw")
@@ -182,7 +187,6 @@ def tile_attend_gpdirect_leaning_kernel(
         fused(left0, rc, k_rc[:], base_sb, ALU.mult, ALU.add)
         fused(right0, rhv, l_2root[:], square, ALU.mult, ALU.add)
         fused(left1, rw, k_rw[:], left0, ALU.mult, ALU.add)
-        halves = (slice(0, I // 2), slice(I // 2, I))
         for cols in halves:
             fused(right1, r, k_r[:], right0, ALU.mult, ALU.add, cols=cols)
         for cols, queue in zip(halves, (nc.sync, nc.scalar)):

@@ -120,21 +120,17 @@ def tile_attend_gpdirect_leaning_kernel(
         load_scales(nc.sync, vs_window, vals_scales)
         l = column("l")
         nc.sync.dma_start(out=l[:], in_=lean)
-        l_plus_1 = column("l_plus_1")
-        nc.gpsimd.tensor_scalar(l_plus_1[:], l[:], 1.0, 1.0, ALU.mult, ALU.add)
-        l_2root = column("l_2root")
-        nc.gpsimd.tensor_scalar(l_2root[:], l[:], 2.0 * ROOT, 0.0, ALU.mult, ALU.add)
 
         q_grouped = interleave("q_grouped", q_raw)
-        base_sb = keep.tile([P, PACK * Q], F32, name="base_sb", tag="q_raw", align_bytes=64)
-        nc.sync.dma_start(out=base_sb[:], in_=base)
         g_grouped = interleave("g_grouped", g_raw)
+        base_sb = keep.tile([P, PACK * Q], F32, name="base_sb", tag="g_raw", align_bytes=64)
+        nc.sync.dma_start(out=base_sb[:], in_=base)
 
         kw = gather("kw", kw_window, U16, "kw", whole)
         ks = gather("ks", ks_window, U8, "ks", whole)
         q_mx = quantize("q", q_grouped)
         a = product("a", q_mx, kw, ks, whole)
-        vw = gather("vw", vw_window, U16, "q_grouped", whole)
+        vw = gather("vw", vw_window, U16, "q_raw", whole)
 
         neg_max = column("neg_max")
         neg_a = wide("neg_a")
@@ -142,7 +138,8 @@ def tile_attend_gpdirect_leaning_kernel(
         p, p_sum = wide("p"), column("p_sum")
         nc.scalar.activation(out=p[:], in_=a[:], func=ACT.Exp, bias=neg_max[:], scale=1.0, accum_out=p_sum[:])
         la = wide("la")
-        nc.scalar.activation(out=la[:], in_=a[:], func=ACT.Copy, scale=l[:])
+        nc.scalar.activation(out=la[:], in_=a[:], func=ACT.Identity, scale=l[:], bias=l[:])
+        l_2root = scaled("l_2root", l, 2.0 * ROOT)
 
         g_mx = quantize("g", g_grouped)
         vs = gather("vs", vs_window, U8, "ks", halves)
@@ -154,9 +151,9 @@ def tile_attend_gpdirect_leaning_kernel(
         nc.scalar.activation(out=r[:], in_=p[:], func=ACT.Copy, scale=inv_sum[:])
 
         rc, c_mean = wide("rc"), column("c_mean")
-        neg_pla = column("neg_pla")
-        fused(rc, neg_a, l[:], p, ALU.mult, ALU.mult, neg_pla)
-        w_shift = affine("w_shift", neg_pla, inv_sum[:], l_plus_1[:])
+        spare, neg_pla = wide("spare"), column("neg_pla")
+        fused(spare, neg_a, l[:], p, ALU.mult, ALU.mult, neg_pla)
+        w_shift = affine("w_shift", neg_pla, inv_sum[:], 1.0)
         fused(rc, c, inv_sum[:], p, ALU.mult, ALU.mult, c_mean)
         rw = wide("rw")
         fused(rw, la, w_shift[:], r, ALU.add, ALU.mult)

import math
from contextlib import ExitStack

import concourse.mybir as mybir

D, E, T, I, Q = 512, 512, 2048, 512, 128
FLOPS = 2 * Q * I * (D + E)

F32 = mybir.dt.float32
BF16 = mybir.dt.bfloat16
I32 = mybir.dt.int32
U32 = mybir.dt.uint32
U16 = mybir.dt.uint16
U8 = mybir.dt.uint8
FP8X4 = mybir.dt.float8_e4m3fn_x4
FP4X4 = mybir.dt.float4_e2m1fn_x4
ALU = mybir.AluOpType
ACT = mybir.ActivationFunctionType

P = 128
PACK = 4
PENALTY = 2.0 * 512.0 * 512.0
ROOT = math.sqrt(PENALTY)


def tile_attend_gpdirect_leaning_kernel(
    tc, query, keys_words, keys_scales, lean, gout, vals_words, vals_scales, base, offs, out
):
    nc = tc.nc
    with ExitStack() as ctx:
        keep = ctx.enter_context(tc.tile_pool(name="keep", bufs=1))
        psum = ctx.enter_context(tc.psum_pool(name="psum", bufs=1))

        def wide(name):
            return keep.tile([P, I], F32, name=name, align_bytes=64)

        def column(name):
            return keep.tile([P, 1], F32, name=name)

        def scale_window(name, engine):
            window = keep.tile([P, T], U8, name=name, align_bytes=64)
            engine.memset(window[:].bitcast(I32), 0)
            return window

        def load_scales(queue, window, scales):
            rows = scales[0].bitcast(I32)
            for quadrant in range(4):
                queue.dma_start(
                    out=window[32 * quadrant : 32 * quadrant + 4, :].bitcast(I32),
                    in_=rows[4 * quadrant : 4 * quadrant + 4, :],
                )

        def load_words(name, words):
            window = keep.tile([P, T], U16, name=name, align_bytes=64)
            nc.sync.dma_start(out=window[:].bitcast(I32), in_=words[0].bitcast(I32))
            return window

        def load_rows(name, rows):
            raw = keep.tile([P, PACK * Q], F32, name=name, tag=name, align_bytes=64)
            nc.sync.dma_start(out=raw[:], in_=rows.rearrange("(p t) q -> p (t q)", t=PACK))
            return raw

        def interleave(name, raw):
            grouped = keep.tile([P, Q, PACK], BF16, name=name, tag=name, align_bytes=64)
            nc.scalar.copy(out=grouped[:], in_=raw[:].rearrange("p (t q) -> p q t", t=PACK))
            return grouped

        def quantize(name, grouped):
            codes = keep.tile([P, Q], U32, name=name + "_codes", align_bytes=64)
            scales = keep.tile([P, Q], U8, name=name + "_scales", align_bytes=64)
            nc.vector.quantize_mx(
                out=codes[:].bitcast(FP8X4), scales=scales[:], in_=grouped[:].rearrange("p q t -> p (q t)")
            )
            return codes, scales

        def gather(name, window, dtype, tag, parts):
            picked = keep.tile([P, I], dtype, name=name, tag=tag, align_bytes=64)
            for cols in parts:
                entries = offsets[:, cols.start // 16 : cols.stop // 16]
                nc.vector.tensor_copy(picked[:, cols], window[:].indirect(entries))
            return picked

        def product(name, rows, words, scales, parts):
            bank = psum.tile([P, I], F32, name=name)
            for cols in parts:
                nc.tensor.matmul_mx(
                    out=bank[:, cols], lhsT=rows[0][:].bitcast(FP8X4), lhsT_scale=rows[1][:],
                    rhs=words[:, cols].bitcast(FP4X4), rhs_scale=scales[:, cols], start=True, stop=True,
                )
            return bank

        def fused(out_tile, in0, scalar, in1, op0, op1, total=None, cols=slice(0, I)):
            nc.vector.scalar_tensor_tensor(
                out=out_tile[:, cols], in0=in0[:, cols], scalar=scalar, in1=in1[:, cols], op0=op0, op1=op1,
                accum_out=None if total is None else total[:],
            )

        def affine(name, x, scale, bias):
            y = column(name)
            nc.scalar.activation(out=y[:], in_=x[:], func=ACT.Identity, scale=scale, bias=bias)
            return y

        def scaled(name, x, scale):
            y = column(name)
            nc.scalar.activation(out=y[:], in_=x[:], func=ACT.Copy, scale=scale)
            return y

        whole = (slice(0, I),)
        halves = (slice(0, I // 2), slice(I // 2, I))
        ks_window = scale_window("ks_window", nc.vector)
        vs_window = scale_window("vs_window", nc.vector)

        offsets = keep.tile([P, I // 16], U16, name="offsets")
        kw_window = load_words("kw_window", keys_words)
        nc.sync.dma_start(offsets[:], offs)
        load_scales(nc.sync, ks_window, keys_scales)
        q_raw = load_rows("q_raw", query)
        vw_window = load_words("vw_window", vals_words)
        g_raw = load_rows("g_raw", gout)
        load_scales(nc.sync, vs_window, vals_scales)
        l = column("l")
        nc.sync.dma_start(out=l[:], in_=lean)

        q_grouped = interleave("q_grouped", q_raw)
        g_grouped = interleave("g_grouped", g_raw)
        base_sb = keep.tile([P, PACK * Q], F32, name="base_sb", tag="g_raw", align_bytes=64)
        nc.sync.dma_start(out=base_sb[:], in_=base)

        kw = gather("kw", kw_window, U16, "kw", whole)
        ks = gather("ks", ks_window, U8, "ks", whole)
        q_mx = quantize("q", q_grouped)
        a = product("a", q_mx, kw, ks, whole)
        vw = gather("vw", vw_window, U16, "q_raw", whole)

        neg_max = column("neg_max")
        neg_a = wide("neg_a")
        nc.vector.tensor_scalar(neg_a[:], a[:], -1.0, None, ALU.mult, ALU.min, accum_out=neg_max[:])
        p, p_sum = wide("p"), column("p_sum")
        nc.scalar.activation(out=p[:], in_=a[:], func=ACT.Exp, bias=neg_max[:], scale=1.0, accum_out=p_sum[:])
        la = wide("la")
        nc.scalar.activation(out=la[:], in_=a[:], func=ACT.Identity, scale=l[:], bias=l[:])
        l_2root = scaled("l_2root", l, 2.0 * ROOT)

        g_mx = quantize("g", g_grouped)
        vs = gather("vs", vs_window, U8, "ks", halves)
        c = product("c", g_mx, vw, vs, halves)

        inv_sum = column("inv_sum")
        nc.vector.reciprocal(out=inv_sum[:], in_=p_sum[:])
        r = wide("r")
        nc.scalar.activation(out=r[:], in_=p[:], func=ACT.Copy, scale=inv_sum[:])

        rc, c_mean = wide("rc"), column("c_mean")
        spare, neg_pla = wide("spare"), column("neg_pla")
        fused(spare, neg_a, l[:], p, ALU.mult, ALU.mult, neg_pla)
        w_shift = affine("w_shift", neg_pla, inv_sum[:], 1.0)
        fused(rc, c, inv_sum[:], p, ALU.mult, ALU.mult, c_mean)
        rw = wide("rw")
        fused(rw, la, w_shift[:], r, ALU.add, ALU.mult)
        rvw, vw_mean = wide("rvw"), column("vw_mean")
        fused(rvw, c, c_mean[:], rw, ALU.subtract, ALU.mult, vw_mean)
        neg_da = wide("neg_da")
        fused(neg_da, r, vw_mean[:], rvw, ALU.mult, ALU.subtract)

        rh, b = wide("rh"), column("b")
        fused(rh, neg_da, -0.5 * ROOT, r, ALU.mult, ALU.mult, b)
        spare2, gh = wide("spare2"), column("gh")
        nc.scalar.activation(out=spare2[:], in_=neg_da[:], func=ACT.Square, scale=ROOT, accum_out=gh[:])
        spare3, neg_hw = wide("spare3"), column("neg_hw")
        fused(spare3, neg_da, PENALTY, rw, ALU.mult, ALU.mult, neg_hw)
        square = wide("square")
        nc.scalar.activation(out=square[:], in_=neg_da[:], func=ACT.Square, scale=ROOT, bias=b[:])
        rhv, hv = wide("rhv"), column("hv")
        fused(rhv, c, c_mean[:], rh, ALU.subtract, ALU.mult, hv)

        k_rc = affine("k_rc", b, 2.0 * ROOT, neg_hw[:])
        t1 = affine("t1", k_rc, c_mean[:], gh[:])
        neg_t1 = scaled("neg_t1", t1, -1.0)
        b_squared = scaled("b_squared", b, b[:])
        k_rw = scaled("k_rw", hv, -2.0 * ROOT)
        k_r = affine("k_r", hv, 2.0 * ROOT, neg_t1[:])

        left0, right0, left1, right1, result = (wide(n) for n in ("left0", "right0", "left1", "right1", "result"))
        fused(left0, rc, k_rc[:], base_sb, ALU.mult, ALU.add)
        fused(right0, rhv, l_2root[:], square, ALU.mult, ALU.add)
        fused(left1, rw, k_rw[:], left0, ALU.mult, ALU.add)
        for cols in halves:
            fused(right1, r, k_r[:], right0, ALU.mult, ALU.add, cols=cols)
        for cols, queue in zip(halves, (nc.sync, nc.scalar)):
            fused(result, left1, b_squared[:], right1, ALU.subtract, ALU.add, cols=cols)
            queue.dma_start(out=out[:, cols], in_=result[:, cols])
